import numpy as np
import ml_dtypes


def mxq(x, axis, fmt="e4m3"):
    dtype, down = {"e4m3": (ml_dtypes.float8_e4m3fn, 7), "e5m2": (ml_dtypes.float8_e5m2, 14)}[fmt]
    v = np.moveaxis(np.asarray(x, np.float32).astype(ml_dtypes.bfloat16).astype(np.float64), axis, -1)
    blocks = v.reshape(v.shape[:-1] + (-1, 32))
    amax = np.abs(blocks).max(-1, keepdims=True)
    byte = np.maximum(np.where(amax > 0, np.frexp(amax)[1] - 1 + 127, 0) - down, 1)
    scale = np.exp2(byte - 127.0)
    codes = (blocks / scale).astype(np.float32).astype(dtype).astype(np.float64)
    return np.moveaxis((codes * scale).reshape(v.shape), -1, axis)


WIDE = False


def mx_kscale(k):
    if not WIDE:
        return np.ones(k)
    levels = np.array([10, -10, 5, -5, 0])
    if k % 512:
        return np.exp2(np.random.permutation(np.resize(levels, k // 32))).repeat(32)
    a = np.empty((k // 512, 16))
    for p in range(k // 512):
        a[p, :8] = np.random.permutation(np.resize(levels, 8))
        for g in range(8):
            far = levels[np.abs(levels - a[p, g]) >= 10]
            a[p, g + 8] = far[np.random.randint(len(far))]
    return np.exp2(a.ravel()).repeat(32)


def f64(x):
    return np.asarray(x).astype(np.float64)


def striped8(idx):
    return np.asarray(idx).reshape(8, -1, 16).transpose(0, 2, 1).reshape(128, -1).astype(np.uint16)


def unstriped8(offs):
    return offs.reshape(8, 16, -1).transpose(0, 2, 1).reshape(8, -1).astype(np.int64)


def pick8(x, idx, run):
    r = np.arange(len(x))
    return x[r[:, None], idx[r % (8 * run) // run]]


E2M1 = np.array([0.0, 0.5, 1.0, 1.5, 2.0, 3.0, 4.0, 6.0, -0.0, -0.5, -1.0, -1.5, -2.0, -3.0, -4.0, -6.0])


def pack_weight(w, fmt):
    k, n = w.shape
    w = f64(np.asarray(w, np.float32).astype(ml_dtypes.bfloat16)).reshape(k // 32, 32, n)
    amax = np.abs(w).max(1)
    if fmt == "e4m3":
        byte = np.frexp(amax)[1] - 1 + 127 - 7
    else:
        mant, ex = np.frexp(amax / 6.0)
        byte = np.where(mant > 0.5, ex, ex - 1) + 127
    byte = np.clip(np.where(amax > 0, byte, 1), 1, 254)
    scaled = (w * np.exp2(127.0 - byte)[:, None, :]).reshape(k, n).astype(np.float32)
    by_word = np.ascontiguousarray(scaled.reshape(k // 512, 128, 4, n).transpose(0, 1, 3, 2))
    if fmt == "e4m3":
        words = by_word.astype(ml_dtypes.float8_e4m3fn).view(np.uint8)
    else:
        c = by_word.astype(ml_dtypes.float4_e2m1fn).view(np.uint8) & 0xF
        words = (c[..., 0::2] | (c[..., 1::2] << 4)).reshape(k // 512, 128, 2 * n)
    return np.ascontiguousarray(words), np.ascontiguousarray(byte.astype(np.uint8).reshape(k // 512, 16, n))


def unpack_weight(words, scales, fmt):
    g, _, n = scales.shape
    words = np.ascontiguousarray(words).reshape(g, 128, n, -1)
    if fmt == "e4m3":
        vals = words.view(ml_dtypes.float8_e4m3fn).astype(np.float64)
    else:
        nib = np.empty((g, 128, n, 4), np.uint8)
        nib[..., 0::2] = words & 0xF
        nib[..., 1::2] = words >> 4
        vals = E2M1[nib]
    vals = vals * np.repeat(np.exp2(scales.astype(np.float64) - 127.0), 8, axis=1)[..., None]
    return vals.transpose(0, 1, 3, 2).reshape(g * 512, n)


D, K, T, U, I, Q = 512, 512, 1024, 1024, 512, 128


def setup_inputs():
    n = np.random.standard_normal
    idx = np.stack([np.random.permutation(T)[:I] for _ in range(8)])
    idx2 = np.stack([np.random.permutation(U)[:I] for _ in range(8)])
    idx3 = np.stack([np.random.permutation(U)[:I] for _ in range(8)])
    idx4 = np.stack([np.random.permutation(U)[:I] for _ in range(8)])
    idx5 = np.stack([np.random.permutation(T)[:I] for _ in range(8)])
    fd = mx_kscale(D)
    fk = mx_kscale(K)
    wqp = pack_weight(n((D, K)) * 1.0 / np.sqrt(D) * fd[:, None] * fk, "e4m3")
    cachep = pack_weight(n((K, T)) * 1.0 / np.sqrt(K) / fk[:, None], "e4m3")
    draftp = pack_weight(n((D, U)) * 1.0 / np.sqrt(D) * fd[:, None], "e2m1")
    return {
        "states": (n((D, Q)) * 0.95 / fd[:, None]).astype(np.float32),
        "wq_words": wqp[0],
        "wq_scales": wqp[1],
        "cache_words": cachep[0],
        "cache_scales": cachep[1],
        "draft_words": draftp[0],
        "draft_scales": draftp[1],
        "offs": striped8(idx),
        "offs2": striped8(idx2),
        "offs3": striped8(idx3),
        "offs4": striped8(idx4),
        "offs5": striped8(idx5),
    }


def reference(states, wq_words, wq_scales, cache_words, cache_scales, draft_words, draft_scales, offs, offs2, offs3, offs4, offs5):
    idx = unstriped8(offs)
    idx2 = unstriped8(offs2)
    idx3 = unstriped8(offs3)
    idx4 = unstriped8(offs4)
    idx5 = unstriped8(offs5)
    wqu = unpack_weight(wq_words, wq_scales, "e4m3")
    cacheu = unpack_weight(cache_words, cache_scales, "e4m3")
    draftu = unpack_weight(draft_words, draft_scales, "e2m1")
    statesq = mxq(f64(states), 0, "e4m3")
    qv = wqu.T @ statesq
    qvq = mxq(qv, 0, "e4m3")
    a = qvq.T @ cacheu
    b = statesq.T @ draftu
    f1 = np.zeros((Q, U))
    f1[np.arange(Q)[:, None], idx2[np.arange(Q) % 128 // 16]] = pick8(a, idx, 16)
    f2 = np.zeros((Q, U))
    f2[np.arange(Q)[:, None], idx3[np.arange(Q) % 128 // 16]] = pick8(a, idx, 16)
    r = f1 - f2
    bb = np.maximum(b, r)
    y = pick8(bb, idx4, 16) - pick8(a, idx5, 16)
    return y

@@ -1,0 +1,176 @@
+from contextlib import ExitStack
+
+import concourse.mybir as mybir
+
+D, K, T, U, I, Q = 512, 512, 1024, 1024, 512, 128
+FLOPS = 2 * Q * (D * K + K * T + D * U)
+
+F32 = mybir.dt.float32
+BF16 = mybir.dt.bfloat16
+I32 = mybir.dt.int32
+U32 = mybir.dt.uint32
+U16 = mybir.dt.uint16
+U8 = mybir.dt.uint8
+FP8X4 = mybir.dt.float8_e4m3fn_x4
+FP4X4 = mybir.dt.float4_e2m1fn_x4
+COPY = mybir.ActivationFunctionType.Copy
+SUB = mybir.AluOpType.subtract
+MAX = mybir.AluOpType.max
+
+P = 128
+PACK = 4
+BANK = 512
+HALF = I // 2
+Q_VECTOR = 80
+A_PIECES = (256, 256, 256, 128, 128)
+A_ON_VECTOR = (True, False, True, False, False)
+
+
+def load_scale_rows(queue, plane, rows):
+    for quad in range(4):
+        queue.dma_start(
+            out=plane[32 * quad : 32 * quad + 4, :].bitcast(I32),
+            in_=rows[4 * quad : 4 * quad + 4, :].bitcast(I32),
+        )
+
+
+def tile_attend_bothsides_side_kernel(
+    tc, states, wq_words, wq_scales, cache_words, cache_scales, draft_words, draft_scales,
+    offs, offs2, offs3, offs4, offs5, out,
+):
+    nc = tc.nc
+    with ExitStack() as ctx:
+        sb = ctx.enter_context(tc.tile_pool(name="sb", bufs=1))
+        ps = ctx.enter_context(tc.psum_pool(name="ps", bufs=1))
+
+        wq_plane_in = sb.tile([P, K], U8, align_bytes=64, name="wq_plane_in")
+        cache_plane = sb.tile([P, T], U8, align_bytes=64, name="cache_plane")
+        draft_plane = sb.tile([P, U], U8, align_bytes=64, name="draft_plane")
+        f1 = sb.tile([P, U], F32, align_bytes=64, name="f1")
+        nc.vector.memset(wq_plane_in[:].bitcast(I32), 0)
+        nc.vector.memset(cache_plane[:].bitcast(I32), 0)
+        nc.vector.memset(draft_plane[:].bitcast(I32), 0)
+        nc.vector.memset(f1[:].bitcast(I32), 0)
+
+        states_in = sb.tile([P, PACK, Q], F32, align_bytes=256, name="states_in")
+        wq_in = [sb.tile([P, K // 2], U32, align_bytes=256, name="wq_in%d" % half) for half in range(2)]
+        cache_codes = sb.tile([P, T], U32, align_bytes=256, name="cache_codes")
+        draft_codes = sb.tile([P, 2 * U], U8, align_bytes=256, name="draft_codes")
+        list1 = sb.tile([P, I // 16], U16, name="list1")
+        list2 = sb.tile([P, I // 16], U16, name="list2")
+        list3 = sb.tile([P, I // 16], U16, name="list3")
+        list4 = sb.tile([P, I // 16], U16, name="list4")
+        list5 = sb.tile([P, I // 16], U16, name="list5")
+
+        nc.sync.dma_start(out=states_in[:], in_=states.rearrange("(p j) q -> p j q", j=PACK))
+        wq_rows = wq_words[0].rearrange("p n r -> p (n r)").bitcast(I32)
+        nc.sync.dma_start(out=wq_in[0][:].bitcast(I32), in_=wq_rows[:, : K // 2])
+        load_scale_rows(nc.sync, wq_plane_in, wq_scales[0])
+        nc.sync.dma_start(out=wq_in[1][:].bitcast(I32), in_=wq_rows[:, K // 2 :])
+        nc.sync.dma_start(
+            out=cache_codes[:].bitcast(I32), in_=cache_words[0].rearrange("p n r -> p (n r)").bitcast(I32)
+        )
+        load_scale_rows(nc.sync, cache_plane, cache_scales[0])
+        nc.sync.dma_start(list1[:], offs)
+        nc.sync.dma_start(list2[:], offs2)
+        nc.sync.dma_start(list3[:], offs3)
+        nc.sync.dma_start(list5[:], offs5)
+        nc.sync.dma_start(out=draft_codes[:].bitcast(I32), in_=draft_words[0].bitcast(I32))
+        load_scale_rows(nc.sync, draft_plane, draft_scales[0])
+        nc.sync.dma_start(list4[:], offs4)
+
+        states_bf = sb.tile([P, Q, PACK], BF16, align_bytes=64, name="states_bf", tag="states_bf_then_f2")
+        states_view = states_in[:].rearrange("p j q -> p q j")
+        nc.vector.tensor_copy(out=states_bf[:, :Q_VECTOR, :], in_=states_view[:, :Q_VECTOR, :])
+        nc.scalar.activation(states_bf[:, Q_VECTOR:, :], states_view[:, Q_VECTOR:, :], COPY)
+
+        wq_plane = sb.tile([P, K], U8, align_bytes=64, name="wq_plane")
+        nc.vector.tensor_copy(
+            out=wq_plane[:].rearrange("p (r m) -> p m r", r=PACK),
+            in_=wq_plane_in[:].rearrange("p (m r) -> p m r", r=PACK),
+        )
+        states_codes = sb.tile([P, Q], U32, align_bytes=64, name="states_codes")
+        states_plane = sb.tile([P, Q], U8, align_bytes=64, name="states_plane")
+        nc.vector.quantize_mx(
+            out=states_codes[:].bitcast(FP8X4), scales=states_plane[:],
+            in_=states_bf[:].rearrange("p q j -> p (q j)"),
+        )
+
+        wq_codes = sb.tile([P, K], U32, align_bytes=64, name="wq_codes")
+        wq_dealt = wq_codes[:].rearrange("p (r m) -> p m r", r=PACK)
+        for half in range(2):
+            nc.scalar.copy(
+                wq_dealt[:, half * P // 2 : (half + 1) * P // 2, :],
+                wq_in[half][:].rearrange("p (m r) -> p m r", r=PACK),
+            )
+
+        qv_bank = ps.tile([P, PACK, Q], F32, name="qv_bank")
+        for r in range(PACK):
+            cols = slice(r * P, (r + 1) * P)
+            nc.tensor.matmul_mx(
+                out=qv_bank[:, r, :], lhsT=wq_codes[:, cols].bitcast(FP8X4), lhsT_scale=wq_plane[:, cols],
+                rhs=states_codes[:].bitcast(FP8X4), rhs_scale=states_plane[:], start=True, stop=True,
+            )
+        qv_bf = sb.tile([P, Q, PACK], BF16, align_bytes=64, name="qv_bf")
+        nc.scalar.copy(qv_bf[:], qv_bank[:].rearrange("p r q -> p q r"))
+        qv_codes = sb.tile([P, Q], U32, align_bytes=64, name="qv_codes")
+        qv_plane = sb.tile([P, Q], U8, align_bytes=64, name="qv_plane")
+        nc.vector.quantize_mx(
+            out=qv_codes[:].bitcast(FP8X4), scales=qv_plane[:], in_=qv_bf[:].rearrange("p q r -> p (q r)")
+        )
+
+        f2 = sb.tile([P, U], F32, align_bytes=64, name="f2", tag="states_bf_then_f2")
+        nc.vector.memset(f2[:].bitcast(I32), 0)
+
+        a = sb.tile([P, T], F32, align_bytes=64, name="a")
+        first = 0
+        for piece, (width, on_vector) in enumerate(zip(A_PIECES, A_ON_VECTOR)):
+            cols = slice(first, first + width)
+            first = first + width
+            a_bank = ps.tile([P, width], F32, name="a_bank%d" % piece)
+            nc.tensor.matmul_mx(
+                out=a_bank[:], lhsT=qv_codes[:].bitcast(FP8X4), lhsT_scale=qv_plane[:],
+                rhs=cache_codes[:, cols].bitcast(FP8X4), rhs_scale=cache_plane[:, cols], start=True, stop=True,
+            )
+            if on_vector:
+                nc.vector.tensor_copy(out=a[:, cols], in_=a_bank[:])
+            else:
+                nc.scalar.copy(a[:, cols], a_bank[:])
+
+        b_banks = []
+        for bank in range(U // BANK):
+            b_bank = ps.tile([P, BANK], F32, name="b_bank%d" % bank)
+            nc.tensor.matmul_mx(
+                out=b_bank[:], lhsT=states_codes[:].bitcast(FP8X4), lhsT_scale=states_plane[:],
+                rhs=draft_codes[:, 2 * bank * BANK : 2 * (bank + 1) * BANK].bitcast(FP4X4),
+                rhs_scale=draft_plane[:, bank * BANK : (bank + 1) * BANK], start=True, stop=True,
+            )
+            b_banks.append(b_bank)
+
+        for half in range(2):
+            entries = slice(half * HALF // 16, (half + 1) * HALF // 16)
+            picked = sb.tile([P, HALF], F32, align_bytes=64, name="picked%d" % half)
+            nc.vector.tensor_copy(out=picked[:], in_=a[:].indirect(list1[:, entries]))
+            nc.scalar.activation(f1[:].indirect(list2[:, entries]), picked[:], COPY)
+            nc.scalar.activation(f2[:].indirect(list3[:, entries]), picked[:], COPY)
+
+        a5 = sb.tile([P, I], F32, align_bytes=64, name="a5")
+        nc.vector.tensor_copy(out=a5[:], in_=a[:].indirect(list5[:]))
+
+        diff = sb.tile([P, U], F32, align_bytes=64, name="diff")
+        bb = sb.tile([P, U], F32, align_bytes=64, name="bb")
+        for bank in range(U // BANK):
+            cols = slice(bank * BANK, (bank + 1) * BANK)
+            nc.vector.tensor_tensor(diff[:, cols], f1[:, cols], f2[:, cols], SUB)
+        for bank in range(U // BANK):
+            cols = slice(bank * BANK, (bank + 1) * BANK)
+            nc.vector.tensor_tensor(bb[:, cols], diff[:, cols], b_banks[bank][:], MAX)
+
+        y0 = sb.tile([P, HALF], F32, align_bytes=64, name="y0")
+        nc.vector.tensor_tensor(y0[:], bb[:].indirect(list4[:, : HALF // 16]), a5[:, :HALF], SUB)
+        nc.sync.dma_start(out=out[:, :HALF], in_=y0[:])
+        bb4 = sb.tile([P, HALF], F32, align_bytes=64, name="bb4")
+        nc.scalar.activation(bb4[:], bb[:].indirect(list4[:, HALF // 16 :]), COPY)
+        y1 = sb.tile([P, HALF], F32, align_bytes=64, name="y1")
+        nc.vector.tensor_tensor(y1[:], bb4[:], a5[:, HALF:], SUB)
+        nc.sync.dma_start(out=out[:, HALF:], in_=y1[:])

@@ -23,7 +23,8 @@ BANK = 512
 HALF = I // 2
 Q_VECTOR = 80
 A_PIECES = (256, 256, 256, 128, 128)
-A_ON_VECTOR = (True, False, True, False, False)
+A_TAGS = ("a0", "a1", "a2", "early0", "early1")
+A_ON_VECTOR = (False, True, False, True, False)
 
 
 def load_scale_rows(queue, plane, rows):
@@ -63,23 +64,21 @@ def tile_attend_bothsides_side_kernel(
         list5 = sb.tile([P, I // 16], U16, name="list5")
 
         nc.sync.dma_start(out=states_in[:], in_=states.rearrange("(p j) q -> p j q", j=PACK))
-        wq_rows = wq_words[0].rearrange("p n r -> p (n r)").bitcast(I32)
-        nc.sync.dma_start(out=wq_in[0][:].bitcast(I32), in_=wq_rows[:, : K // 2])
         load_scale_rows(nc.sync, wq_plane_in, wq_scales[0])
-        nc.sync.dma_start(out=wq_in[1][:].bitcast(I32), in_=wq_rows[:, K // 2 :])
+        wq_rows = wq_words[0].rearrange("p n r -> p (n r)").bitcast(I32)
+        for half in range(2):
+            nc.sync.dma_start(out=wq_in[half][:].bitcast(I32), in_=wq_rows[:, half * K // 2 : (half + 1) * K // 2])
         nc.sync.dma_start(
             out=cache_codes[:].bitcast(I32), in_=cache_words[0].rearrange("p n r -> p (n r)").bitcast(I32)
         )
         load_scale_rows(nc.sync, cache_plane, cache_scales[0])
-        nc.sync.dma_start(list1[:], offs)
-        nc.sync.dma_start(list2[:], offs2)
-        nc.sync.dma_start(list3[:], offs3)
-        nc.sync.dma_start(list5[:], offs5)
+        for tile, source in ((list1, offs), (list2, offs2), (list3, offs3), (list5, offs5)):
+            nc.sync.dma_start(tile[:], source)
         nc.sync.dma_start(out=draft_codes[:].bitcast(I32), in_=draft_words[0].bitcast(I32))
         load_scale_rows(nc.sync, draft_plane, draft_scales[0])
         nc.sync.dma_start(list4[:], offs4)
 
-        states_bf = sb.tile([P, Q, PACK], BF16, align_bytes=64, name="states_bf", tag="states_bf_then_f2")
+        states_bf = sb.tile([P, Q, PACK], BF16, align_bytes=64, name="states_bf")
         states_view = states_in[:].rearrange("p j q -> p q j")
         nc.vector.tensor_copy(out=states_bf[:, :Q_VECTOR, :], in_=states_view[:, :Q_VECTOR, :])
         nc.scalar.activation(states_bf[:, Q_VECTOR:, :], states_view[:, Q_VECTOR:, :], COPY)
@@ -104,30 +103,31 @@ def tile_attend_bothsides_side_kernel(
                 wq_in[half][:].rearrange("p (m r) -> p m r", r=PACK),
             )
 
-        qv_bank = ps.tile([P, PACK, Q], F32, name="qv_bank")
+        qv_banks = [ps.tile([P, 2, Q], F32, name="qv_bank%d" % pair, tag="early%d" % pair) for pair in range(2)]
         for r in range(PACK):
             cols = slice(r * P, (r + 1) * P)
             nc.tensor.matmul_mx(
-                out=qv_bank[:, r, :], lhsT=wq_codes[:, cols].bitcast(FP8X4), lhsT_scale=wq_plane[:, cols],
+                out=qv_banks[r // 2][:, r % 2, :], lhsT=wq_codes[:, cols].bitcast(FP8X4), lhsT_scale=wq_plane[:, cols],
                 rhs=states_codes[:].bitcast(FP8X4), rhs_scale=states_plane[:], start=True, stop=True,
             )
-        qv_bf = sb.tile([P, Q, PACK], BF16, align_bytes=64, name="qv_bf")
-        nc.scalar.copy(qv_bf[:], qv_bank[:].rearrange("p r q -> p q r"))
+        qv_bf = sb.tile([P, Q, PACK], BF16, align_bytes=64, name="qv_bf", tag="qv_bf_then_f2")
+        nc.vector.tensor_copy(out=qv_bf[:, :, 0:2], in_=qv_banks[0][:].rearrange("p r q -> p q r"))
+        nc.scalar.copy(qv_bf[:, :, 2:4], qv_banks[1][:].rearrange("p r q -> p q r"))
         qv_codes = sb.tile([P, Q], U32, align_bytes=64, name="qv_codes")
         qv_plane = sb.tile([P, Q], U8, align_bytes=64, name="qv_plane")
         nc.vector.quantize_mx(
             out=qv_codes[:].bitcast(FP8X4), scales=qv_plane[:], in_=qv_bf[:].rearrange("p q r -> p (q r)")
         )
 
-        f2 = sb.tile([P, U], F32, align_bytes=64, name="f2", tag="states_bf_then_f2")
-        nc.vector.memset(f2[:].bitcast(I32), 0)
+        f2 = sb.tile([P, U], F32, align_bytes=64, name="f2", tag="qv_bf_then_f2")
+        nc.gpsimd.memset(f2[:].bitcast(I32), 0)
 
         a = sb.tile([P, T], F32, align_bytes=64, name="a")
         first = 0
         for piece, (width, on_vector) in enumerate(zip(A_PIECES, A_ON_VECTOR)):
             cols = slice(first, first + width)
             first = first + width
-            a_bank = ps.tile([P, width], F32, name="a_bank%d" % piece)
+            a_bank = ps.tile([P, width], F32, name="a_bank%d" % piece, tag=A_TAGS[piece])
             nc.tensor.matmul_mx(
                 out=a_bank[:], lhsT=qv_codes[:].bitcast(FP8X4), lhsT_scale=qv_plane[:],
                 rhs=cache_codes[:, cols].bitcast(FP8X4), rhs_scale=cache_plane[:, cols], start=True, stop=True,

@@ -84,10 +84,9 @@ def tile_attend_bothsides_side_kernel(
         nc.scalar.activation(states_bf[:, Q_VECTOR:, :], states_view[:, Q_VECTOR:, :], COPY)
 
         wq_plane = sb.tile([P, K], U8, align_bytes=64, name="wq_plane")
-        nc.vector.tensor_copy(
-            out=wq_plane[:].rearrange("p (r m) -> p m r", r=PACK),
-            in_=wq_plane_in[:].rearrange("p (m r) -> p m r", r=PACK),
-        )
+        plane_dealt = wq_plane[:].rearrange("p (r m) -> p m r", r=PACK)
+        plane_given = wq_plane_in[:].rearrange("p (m r) -> p m r", r=PACK)
+        nc.vector.tensor_copy(out=plane_dealt[:, :, 0:2], in_=plane_given[:, :, 0:2])
         states_codes = sb.tile([P, Q], U32, align_bytes=64, name="states_codes")
         states_plane = sb.tile([P, Q], U8, align_bytes=64, name="states_plane")
         nc.vector.quantize_mx(
@@ -95,13 +94,15 @@ def tile_attend_bothsides_side_kernel(
             in_=states_bf[:].rearrange("p q j -> p (q j)"),
         )
 
+        nc.vector.tensor_copy(out=plane_dealt[:, :, 2:4], in_=plane_given[:, :, 2:4])
+
         wq_codes = sb.tile([P, K], U32, align_bytes=64, name="wq_codes")
         wq_dealt = wq_codes[:].rearrange("p (r m) -> p m r", r=PACK)
-        for half in range(2):
-            nc.scalar.copy(
-                wq_dealt[:, half * P // 2 : (half + 1) * P // 2, :],
-                wq_in[half][:].rearrange("p (m r) -> p m r", r=PACK),
-            )
+        wq_given = [tile[:].rearrange("p (m r) -> p m r", r=PACK) for tile in wq_in]
+        nc.scalar.copy(wq_dealt[:, : P // 2, :], wq_given[0])
+        for pair in range(2):
+            places = slice(2 * pair, 2 * pair + 2)
+            nc.scalar.copy(wq_dealt[:, P // 2 :, places], wq_given[1][:, :, places])
 
         qv_banks = [ps.tile([P, 2, Q], F32, name="qv_bank%d" % pair, tag="early%d" % pair) for pair in range(2)]
         for r in range(PACK):

from contextlib import ExitStack

import concourse.mybir as mybir

D, K, T, U, I, Q = 512, 512, 1024, 1024, 512, 128
FLOPS = 2 * Q * (D * K + K * T + D * U)

F32 = mybir.dt.float32
BF16 = mybir.dt.bfloat16
I32 = mybir.dt.int32
U32 = mybir.dt.uint32
U16 = mybir.dt.uint16
U8 = mybir.dt.uint8
FP8X4 = mybir.dt.float8_e4m3fn_x4
FP4X4 = mybir.dt.float4_e2m1fn_x4
COPY = mybir.ActivationFunctionType.Copy
SUB = mybir.AluOpType.subtract
MAX = mybir.AluOpType.max

P = 128
PACK = 4
BANK = 512
HALF = I // 2
Q_VECTOR = 80
A_PIECES = (256, 256, 256, 128, 128)
A_TAGS = ("a0", "a1", "a2", "early0", "early1")
A_ON_VECTOR = (False, True, False, True, False)


def load_scale_rows(queue, plane, rows):
    for quad in range(4):
        queue.dma_start(
            out=plane[32 * quad : 32 * quad + 4, :].bitcast(I32),
            in_=rows[4 * quad : 4 * quad + 4, :].bitcast(I32),
        )


def tile_attend_bothsides_side_kernel(
    tc, states, wq_words, wq_scales, cache_words, cache_scales, draft_words, draft_scales,
    offs, offs2, offs3, offs4, offs5, out,
):
    nc = tc.nc
    with ExitStack() as ctx:
        sb = ctx.enter_context(tc.tile_pool(name="sb", bufs=1))
        ps = ctx.enter_context(tc.psum_pool(name="ps", bufs=1))

        wq_plane_in = sb.tile([P, K], U8, align_bytes=64, name="wq_plane_in")
        cache_plane = sb.tile([P, T], U8, align_bytes=64, name="cache_plane")
        draft_plane = sb.tile([P, U], U8, align_bytes=64, name="draft_plane")
        f1 = sb.tile([P, U], F32, align_bytes=64, name="f1")
        nc.vector.memset(wq_plane_in[:].bitcast(I32), 0)
        nc.vector.memset(cache_plane[:].bitcast(I32), 0)
        nc.vector.memset(draft_plane[:].bitcast(I32), 0)
        nc.vector.memset(f1[:].bitcast(I32), 0)

        states_in = sb.tile([P, PACK, Q], F32, align_bytes=256, name="states_in")
        wq_in = [sb.tile([P, K // 2], U32, align_bytes=256, name="wq_in%d" % half) for half in range(2)]
        cache_codes = sb.tile([P, T], U32, align_bytes=256, name="cache_codes")
        draft_codes = sb.tile([P, 2 * U], U8, align_bytes=256, name="draft_codes")
        list1 = sb.tile([P, I // 16], U16, name="list1")
        list2 = sb.tile([P, I // 16], U16, name="list2")
        list3 = sb.tile([P, I // 16], U16, name="list3")
        list4 = sb.tile([P, I // 16], U16, name="list4")
        list5 = sb.tile([P, I // 16], U16, name="list5")

        nc.sync.dma_start(out=states_in[:], in_=states.rearrange("(p j) q -> p j q", j=PACK))
        load_scale_rows(nc.sync, wq_plane_in, wq_scales[0])
        wq_rows = wq_words[0].rearrange("p n r -> p (n r)").bitcast(I32)
        for half in range(2):
            nc.sync.dma_start(out=wq_in[half][:].bitcast(I32), in_=wq_rows[:, half * K // 2 : (half + 1) * K // 2])
        nc.sync.dma_start(
            out=cache_codes[:].bitcast(I32), in_=cache_words[0].rearrange("p n r -> p (n r)").bitcast(I32)
        )
        load_scale_rows(nc.sync, cache_plane, cache_scales[0])
        for tile, source in ((list1, offs), (list2, offs2), (list3, offs3), (list5, offs5)):
            nc.sync.dma_start(tile[:], source)
        nc.sync.dma_start(out=draft_codes[:].bitcast(I32), in_=draft_words[0].bitcast(I32))
        load_scale_rows(nc.sync, draft_plane, draft_scales[0])
        nc.sync.dma_start(list4[:], offs4)

        states_bf = sb.tile([P, Q, PACK], BF16, align_bytes=64, name="states_bf")
        states_view = states_in[:].rearrange("p j q -> p q j")
        nc.vector.tensor_copy(out=states_bf[:, :Q_VECTOR, :], in_=states_view[:, :Q_VECTOR, :])
        nc.scalar.activation(states_bf[:, Q_VECTOR:, :], states_view[:, Q_VECTOR:, :], COPY)

        wq_plane = sb.tile([P, K], U8, align_bytes=64, name="wq_plane")
        plane_dealt = wq_plane[:].rearrange("p (r m) -> p m r", r=PACK)
        plane_given = wq_plane_in[:].rearrange("p (m r) -> p m r", r=PACK)
        nc.vector.tensor_copy(out=plane_dealt[:, :, 0:2], in_=plane_given[:, :, 0:2])
        states_codes = sb.tile([P, Q], U32, align_bytes=64, name="states_codes")
        states_plane = sb.tile([P, Q], U8, align_bytes=64, name="states_plane")
        nc.vector.quantize_mx(
            out=states_codes[:].bitcast(FP8X4), scales=states_plane[:],
            in_=states_bf[:].rearrange("p q j -> p (q j)"),
        )

        nc.vector.tensor_copy(out=plane_dealt[:, :, 2:4], in_=plane_given[:, :, 2:4])

        wq_codes = sb.tile([P, K], U32, align_bytes=64, name="wq_codes")
        wq_dealt = wq_codes[:].rearrange("p (r m) -> p m r", r=PACK)
        wq_given = [tile[:].rearrange("p (m r) -> p m r", r=PACK) for tile in wq_in]
        nc.scalar.copy(wq_dealt[:, : P // 2, :], wq_given[0])
        for pair in range(2):
            places = slice(2 * pair, 2 * pair + 2)
            nc.scalar.copy(wq_dealt[:, P // 2 :, places], wq_given[1][:, :, places])

        qv_banks = [ps.tile([P, 2, Q], F32, name="qv_bank%d" % pair, tag="early%d" % pair) for pair in range(2)]
        for r in range(PACK):
            cols = slice(r * P, (r + 1) * P)
            nc.tensor.matmul_mx(
                out=qv_banks[r // 2][:, r % 2, :], lhsT=wq_codes[:, cols].bitcast(FP8X4), lhsT_scale=wq_plane[:, cols],
                rhs=states_codes[:].bitcast(FP8X4), rhs_scale=states_plane[:], start=True, stop=True,
            )
        qv_bf = sb.tile([P, Q, PACK], BF16, align_bytes=64, name="qv_bf", tag="qv_bf_then_f2")
        nc.vector.tensor_copy(out=qv_bf[:, :, 0:2], in_=qv_banks[0][:].rearrange("p r q -> p q r"))
        nc.scalar.copy(qv_bf[:, :, 2:4], qv_banks[1][:].rearrange("p r q -> p q r"))
        qv_codes = sb.tile([P, Q], U32, align_bytes=64, name="qv_codes")
        qv_plane = sb.tile([P, Q], U8, align_bytes=64, name="qv_plane")
        nc.vector.quantize_mx(
            out=qv_codes[:].bitcast(FP8X4), scales=qv_plane[:], in_=qv_bf[:].rearrange("p q r -> p (q r)")
        )

        f2 = sb.tile([P, U], F32, align_bytes=64, name="f2", tag="qv_bf_then_f2")
        nc.gpsimd.memset(f2[:].bitcast(I32), 0)

        a = sb.tile([P, T], F32, align_bytes=64, name="a")
        first = 0
        for piece, (width, on_vector) in enumerate(zip(A_PIECES, A_ON_VECTOR)):
            cols = slice(first, first + width)
            first = first + width
            a_bank = ps.tile([P, width], F32, name="a_bank%d" % piece, tag=A_TAGS[piece])
            nc.tensor.matmul_mx(
                out=a_bank[:], lhsT=qv_codes[:].bitcast(FP8X4), lhsT_scale=qv_plane[:],
                rhs=cache_codes[:, cols].bitcast(FP8X4), rhs_scale=cache_plane[:, cols], start=True, stop=True,
            )
            if on_vector:
                nc.vector.tensor_copy(out=a[:, cols], in_=a_bank[:])
            else:
                nc.scalar.copy(a[:, cols], a_bank[:])

        b_banks = []
        for bank in range(U // BANK):
            b_bank = ps.tile([P, BANK], F32, name="b_bank%d" % bank)
            nc.tensor.matmul_mx(
                out=b_bank[:], lhsT=states_codes[:].bitcast(FP8X4), lhsT_scale=states_plane[:],
                rhs=draft_codes[:, 2 * bank * BANK : 2 * (bank + 1) * BANK].bitcast(FP4X4),
                rhs_scale=draft_plane[:, bank * BANK : (bank + 1) * BANK], start=True, stop=True,
            )
            b_banks.append(b_bank)

        for half in range(2):
            entries = slice(half * HALF // 16, (half + 1) * HALF // 16)
            picked = sb.tile([P, HALF], F32, align_bytes=64, name="picked%d" % half)
            nc.vector.tensor_copy(out=picked[:], in_=a[:].indirect(list1[:, entries]))
            nc.scalar.activation(f1[:].indirect(list2[:, entries]), picked[:], COPY)
            nc.scalar.activation(f2[:].indirect(list3[:, entries]), picked[:], COPY)

        a5 = sb.tile([P, I], F32, align_bytes=64, name="a5")
        nc.vector.tensor_copy(out=a5[:], in_=a[:].indirect(list5[:]))

        diff = sb.tile([P, U], F32, align_bytes=64, name="diff")
        bb = sb.tile([P, U], F32, align_bytes=64, name="bb")
        for bank in range(U // BANK):
            cols = slice(bank * BANK, (bank + 1) * BANK)
            nc.vector.tensor_tensor(diff[:, cols], f1[:, cols], f2[:, cols], SUB)
        for bank in range(U // BANK):
            cols = slice(bank * BANK, (bank + 1) * BANK)
            nc.vector.tensor_tensor(bb[:, cols], diff[:, cols], b_banks[bank][:], MAX)

        y0 = sb.tile([P, HALF], F32, align_bytes=64, name="y0")
        nc.vector.tensor_tensor(y0[:], bb[:].indirect(list4[:, : HALF // 16]), a5[:, :HALF], SUB)
        nc.sync.dma_start(out=out[:, :HALF], in_=y0[:])
        bb4 = sb.tile([P, HALF], F32, align_bytes=64, name="bb4")
        nc.scalar.activation(bb4[:], bb[:].indirect(list4[:, HALF // 16 :]), COPY)
        y1 = sb.tile([P, HALF], F32, align_bytes=64, name="y1")
        nc.vector.tensor_tensor(y1[:], bb4[:], a5[:, HALF:], SUB)
        nc.sync.dma_start(out=out[:, HALF:], in_=y1[:])
